import numpy as np
import ml_dtypes


def mxq(x, axis, fmt="e4m3"):
    dtype, down = {"e4m3": (ml_dtypes.float8_e4m3fn, 7), "e5m2": (ml_dtypes.float8_e5m2, 14)}[fmt]
    v = np.moveaxis(np.asarray(x, np.float32).astype(ml_dtypes.bfloat16).astype(np.float64), axis, -1)
    blocks = v.reshape(v.shape[:-1] + (-1, 32))
    amax = np.abs(blocks).max(-1, keepdims=True)
    byte = np.maximum(np.where(amax > 0, np.frexp(amax)[1] - 1 + 127, 0) - down, 1)
    scale = np.exp2(byte - 127.0)
    codes = (blocks / scale).astype(np.float32).astype(dtype).astype(np.float64)
    return np.moveaxis((codes * scale).reshape(v.shape), -1, axis)


WIDE = False


def mx_kscale(k):
    if not WIDE:
        return np.ones(k)
    levels = np.array([10, -10, 5, -5, 0])
    if k % 512:
        return np.exp2(np.random.permutation(np.resize(levels, k // 32))).repeat(32)
    a = np.empty((k // 512, 16))
    for p in range(k // 512):
        a[p, :8] = np.random.permutation(np.resize(levels, 8))
        for g in range(8):
            far = levels[np.abs(levels - a[p, g]) >= 10]
            a[p, g + 8] = far[np.random.randint(len(far))]
    return np.exp2(a.ravel()).repeat(32)


def f64(x):
    return np.asarray(x).astype(np.float64)


def striped8(idx):
    return np.asarray(idx).reshape(8, -1, 16).transpose(0, 2, 1).reshape(128, -1).astype(np.uint16)


def unstriped8(offs):
    return offs.reshape(8, 16, -1).transpose(0, 2, 1).reshape(8, -1).astype(np.int64)


def pick8(x, idx, run):
    r = np.arange(len(x))
    return x[r[:, None], idx[r % (8 * run) // run]]


E2M1 = np.array([0.0, 0.5, 1.0, 1.5, 2.0, 3.0, 4.0, 6.0, -0.0, -0.5, -1.0, -1.5, -2.0, -3.0, -4.0, -6.0])


def pack_weight(w, fmt):
    k, n = w.shape
    w = f64(np.asarray(w, np.float32).astype(ml_dtypes.bfloat16)).reshape(k // 32, 32, n)
    amax = np.abs(w).max(1)
    if fmt == "e4m3":
        byte = np.frexp(amax)[1] - 1 + 127 - 7
    else:
        mant, ex = np.frexp(amax / 6.0)
        byte = np.where(mant > 0.5, ex, ex - 1) + 127
    byte = np.clip(np.where(amax > 0, byte, 1), 1, 254)
    scaled = (w * np.exp2(127.0 - byte)[:, None, :]).reshape(k, n).astype(np.float32)
    by_word = np.ascontiguousarray(scaled.reshape(k // 512, 128, 4, n).transpose(0, 1, 3, 2))
    if fmt == "e4m3":
        words = by_word.astype(ml_dtypes.float8_e4m3fn).view(np.uint8)
    else:
        c = by_word.astype(ml_dtypes.float4_e2m1fn).view(np.uint8) & 0xF
        words = (c[..., 0::2] | (c[..., 1::2] << 4)).reshape(k // 512, 128, 2 * n)
    return np.ascontiguousarray(words), np.ascontiguousarray(byte.astype(np.uint8).reshape(k // 512, 16, n))


def unpack_weight(words, scales, fmt):
    g, _, n = scales.shape
    words = np.ascontiguousarray(words).reshape(g, 128, n, -1)
    if fmt == "e4m3":
        vals = words.view(ml_dtypes.float8_e4m3fn).astype(np.float64)
    else:
        nib = np.empty((g, 128, n, 4), np.uint8)
        nib[..., 0::2] = words & 0xF
        nib[..., 1::2] = words >> 4
        vals = E2M1[nib]
    vals = vals * np.repeat(np.exp2(scales.astype(np.float64) - 127.0), 8, axis=1)[..., None]
    return vals.transpose(0, 1, 3, 2).reshape(g * 512, n)


D, T, I, Q = 512, 1024, 512, 128


def setup_inputs():
    n = np.random.standard_normal
    idx = np.stack([np.random.permutation(T)[:I] for _ in range(8)])
    idx2 = np.stack([np.random.permutation(T)[:I] for _ in range(8)])
    idx3 = np.stack([np.random.permutation(T)[:I] for _ in range(8)])
    fd = mx_kscale(D)
    keysp = pack_weight(n((D, T)) / fd[:, None], "e2m1")
    return {
        "query": (n((D, Q)) * 1.0 / np.sqrt(D) * fd[:, None]).astype(np.float32),
        "keys_words": keysp[0],
        "keys_scales": keysp[1],
        "old": (1.0 * n((Q, T))).astype(np.float32),
        "offs": striped8(idx),
        "offs2": striped8(idx2),
        "offs3": striped8(idx3),
    }


def reference(query, keys_words, keys_scales, old, offs, offs2, offs3):
    idx = unstriped8(offs)
    idx2 = unstriped8(offs2)
    idx3 = unstriped8(offs3)
    keysu = unpack_weight(keys_words, keys_scales, "e2m1")
    queryq = mxq(f64(query), 0, "e4m3")
    a = queryq.T @ keysu
    w = pick8(a, idx, 16) * pick8(a, idx2, 16)
    f1 = np.zeros((Q, T))
    f1[np.arange(Q)[:, None], idx[np.arange(Q) % 128 // 16]] = w
    f2 = f1 + f64(old)
    y = pick8(f2, idx3, 16)
    return y

@@ -1,0 +1,101 @@
+from contextlib import ExitStack
+
+import concourse.mybir as mybir
+
+D, T, I, Q = 512, 1024, 512, 128
+FLOPS = 2 * D * Q * T
+
+F32 = mybir.dt.float32
+BF16 = mybir.dt.bfloat16
+I32 = mybir.dt.int32
+U32 = mybir.dt.uint32
+U16 = mybir.dt.uint16
+U8 = mybir.dt.uint8
+FP8X4 = mybir.dt.float8_e4m3fn_x4
+FP4X4 = mybir.dt.float4_e2m1fn_x4
+COPY = mybir.ActivationFunctionType.Copy
+MULT = mybir.AluOpType.mult
+ADD = mybir.AluOpType.add
+
+P = 128
+PACK = 4
+HALF = I // 2
+N_TILE = 256
+
+
+def tile_attend_pairproduct_lean_through_heads_kernel(tc, query, keys_words, keys_scales, old, offs, offs2, offs3, out):
+    nc = tc.nc
+    with ExitStack() as ctx:
+        lists = ctx.enter_context(tc.tile_pool(name="lists", bufs=1))
+        sb = ctx.enter_context(tc.tile_pool(name="sb", bufs=1))
+        psum = ctx.enter_context(tc.psum_pool(name="psum", bufs=1))
+
+        k_scales = sb.tile([P, T], U8, align_bytes=64)
+        nc.vector.memset(k_scales[:].bitcast(I32), 0)
+        f1 = sb.tile([P, T], F32)
+        nc.vector.memset(f1[:], 0.0)
+
+        q_raw = sb.tile([P, PACK, Q], F32, tag="staged", align_bytes=64)
+        nc.sync.dma_start(out=q_raw[:], in_=query.rearrange("(p j) q -> p j q", j=PACK))
+        for quad in range(4):
+            nc.scalar.dma_start(
+                out=k_scales[32 * quad : 32 * quad + 4, :].bitcast(I32),
+                in_=keys_scales[0, 4 * quad : 4 * quad + 4, :].bitcast(I32),
+            )
+        k_words = sb.tile([P, 2 * T], U8, align_bytes=64)
+        nc.sync.dma_start(out=k_words[:].bitcast(I32), in_=keys_words[0].bitcast(I32))
+        idx = lists.tile([P, I // 16], U16)
+        idx2 = lists.tile([P, I // 16], U16)
+        idx3 = lists.tile([P, I // 16], U16)
+        nc.sync.dma_start(idx[:], offs)
+        nc.sync.dma_start(idx2[:], offs2)
+        nc.sync.dma_start(idx3[:], offs3)
+
+        q_bf = sb.tile([P, Q, PACK], BF16, align_bytes=64)
+        nc.vector.tensor_copy(out=q_bf[:], in_=q_raw[:].rearrange("p j q -> p q j"))
+        q_codes = sb.tile([P, Q], U32, align_bytes=64)
+        q_scales = sb.tile([P, Q], U8, align_bytes=64)
+        nc.vector.quantize_mx(out=q_codes[:].bitcast(FP8X4), scales=q_scales[:], in_=q_bf[:].rearrange("p q j -> p (q j)"))
+
+        old_sb = sb.tile([P, T], F32, tag="staged", align_bytes=64)
+        nc.sync.dma_start(out=old_sb[:], in_=old)
+
+        a = sb.tile([P, T], F32)
+        for n in range(T // N_TILE):
+            cols = slice(n * N_TILE, (n + 1) * N_TILE)
+            bank = psum.tile([P, N_TILE], F32, name=f"bank{n}")
+            nc.tensor.matmul_mx(
+                out=bank[:],
+                lhsT=q_codes[:].bitcast(FP8X4),
+                lhsT_scale=q_scales[:],
+                rhs=k_words[:, 2 * n * N_TILE : 2 * (n + 1) * N_TILE].bitcast(FP4X4),
+                rhs_scale=k_scales[:, cols],
+                start=True,
+                stop=True,
+            )
+            if n % 2 == 0:
+                nc.scalar.activation(a[:, cols], bank[:], COPY)
+            else:
+                nc.vector.tensor_copy(out=a[:, cols], in_=bank[:])
+
+        first, second = slice(0, HALF // 16), slice(HALF // 16, I // 16)
+        u0 = sb.tile([P, HALF], F32)
+        v0 = sb.tile([P, HALF], F32)
+        u1 = sb.tile([P, HALF], F32)
+        v1 = sb.tile([P, HALF], F32)
+        nc.vector.tensor_copy(u0[:], a[:].indirect(idx[:, first]))
+        nc.scalar.activation(v0[:], a[:].indirect(idx2[:, first]), COPY)
+        nc.scalar.activation(u1[:], a[:].indirect(idx[:, second]), COPY)
+        nc.scalar.activation(v1[:], a[:].indirect(idx2[:, second]), COPY)
+        nc.vector.tensor_tensor(f1[:].indirect(idx[:, first]), u0[:], v0[:], MULT)
+        nc.vector.tensor_tensor(f1[:].indirect(idx[:, second]), u1[:], v1[:], MULT)
+
+        f2 = sb.tile([P, T], F32)
+        nc.vector.tensor_tensor(f2[:], f1[:], old_sb[:], ADD)
+
+        y0 = sb.tile([P, HALF], F32)
+        y1 = sb.tile([P, HALF], F32)
+        nc.vector.tensor_copy(y0[:], f2[:].indirect(idx3[:, first]))
+        nc.scalar.activation(y1[:], f2[:].indirect(idx3[:, second]), COPY)
+        nc.sync.dma_start(out=out[:, 0:HALF], in_=y0[:])
+        nc.scalar.dma_start(out=out[:, HALF:I], in_=y1[:])

@@ -1,6 +1,7 @@
 from contextlib import ExitStack
 
 import concourse.mybir as mybir
+from concourse.masks import make_identity
 
 D, T, I, Q = 512, 1024, 512, 128
 FLOPS = 2 * D * Q * T
@@ -20,7 +21,7 @@ ADD = mybir.AluOpType.add
 P = 128
 PACK = 4
 HALF = I // 2
-N_TILE = 256
+V_COLS = 768
 
 
 def tile_attend_pairproduct_lean_through_heads_kernel(tc, query, keys_words, keys_scales, old, offs, offs2, offs3, out):
@@ -51,29 +52,40 @@ def tile_attend_pairproduct_lean_through_heads_kernel(tc, query, keys_words, key
         nc.sync.dma_start(idx2[:], offs2)
         nc.sync.dma_start(idx3[:], offs3)
 
-        q_bf = sb.tile([P, Q, PACK], BF16, align_bytes=64)
-        nc.vector.tensor_copy(out=q_bf[:], in_=q_raw[:].rearrange("p j q -> p q j"))
+        q_bf = sb.tile([P, Q, PACK], BF16, tag="small", align_bytes=64)
         q_codes = sb.tile([P, Q], U32, align_bytes=64)
         q_scales = sb.tile([P, Q], U8, align_bytes=64)
-        nc.vector.quantize_mx(out=q_codes[:].bitcast(FP8X4), scales=q_scales[:], in_=q_bf[:].rearrange("p q j -> p (q j)"))
+        for h in range(2):
+            rows = slice(h * Q // 2, (h + 1) * Q // 2)
+            nc.vector.tensor_copy(
+                out=q_bf[:, rows, :].rearrange("p (c i) j -> p c j i", i=4),
+                in_=q_raw[:, :, rows].rearrange("p j (c i) -> p c j i", i=4),
+            )
+        for h in range(2):
+            rows = slice(h * Q // 2, (h + 1) * Q // 2)
+            nc.vector.quantize_mx(
+                out=q_codes[:, rows].bitcast(FP8X4),
+                scales=q_scales[:, rows],
+                in_=q_bf[:, rows, :].rearrange("p q j -> p (q j)"),
+            )
 
         old_sb = sb.tile([P, T], F32, tag="staged", align_bytes=64)
         nc.sync.dma_start(out=old_sb[:], in_=old)
 
         a = sb.tile([P, T], F32)
-        for n in range(T // N_TILE):
-            cols = slice(n * N_TILE, (n + 1) * N_TILE)
-            bank = psum.tile([P, N_TILE], F32, name=f"bank{n}")
+        for n, (c0, c1) in enumerate(((0, 256), (256, 512), (512, 768), (768, 896), (896, 1024))):
+            cols = slice(c0, c1)
+            bank = psum.tile([P, c1 - c0], F32, name=f"bank{n}", tag=f"bank{n}")
             nc.tensor.matmul_mx(
                 out=bank[:],
                 lhsT=q_codes[:].bitcast(FP8X4),
                 lhsT_scale=q_scales[:],
-                rhs=k_words[:, 2 * n * N_TILE : 2 * (n + 1) * N_TILE].bitcast(FP4X4),
+                rhs=k_words[:, 2 * c0 : 2 * c1].bitcast(FP4X4),
                 rhs_scale=k_scales[:, cols],
                 start=True,
                 stop=True,
             )
-            if n % 2 == 0:
+            if n in (0, 2):
                 nc.scalar.activation(a[:, cols], bank[:], COPY)
             else:
                 nc.vector.tensor_copy(out=a[:, cols], in_=bank[:])
@@ -90,8 +102,25 @@ def tile_attend_pairproduct_lean_through_heads_kernel(tc, query, keys_words, key
         nc.vector.tensor_tensor(f1[:].indirect(idx[:, first]), u0[:], v0[:], MULT)
         nc.vector.tensor_tensor(f1[:].indirect(idx[:, second]), u1[:], v1[:], MULT)
 
+        ident = sb.tile([P, P], F32, tag="small", align_bytes=64)
+        make_identity(nc, ident[:])
+        old_t = sb.tile([P, V_COLS], F32)
+        old_ps = []
+        for b, (c0, c1) in enumerate(((0, 512), (512, V_COLS))):
+            turned = psum.tile([P, c1 - c0], F32, name=f"turned{b}", tag=f"bank{b}")
+            for c in range(c0, c1, P):
+                nc.tensor.transpose(turned[:, c - c0 : c - c0 + P], old_sb[:, c : c + P], ident[:])
+            nc.scalar.copy(old_t[:, c0:c1], turned[:])
+        for b, (c0, c1) in enumerate(((0, 512), (512, V_COLS))):
+            back = psum.tile([P, c1 - c0], F32, name=f"back{b}", tag=f"bank{2 + b}")
+            for c in range(c0, c1, P):
+                nc.tensor.transpose(back[:, c - c0 : c - c0 + P], old_t[:, c : c + P], ident[:])
+            old_ps.append((c0, c1, back))
+
         f2 = sb.tile([P, T], F32)
-        nc.vector.tensor_tensor(f2[:], f1[:], old_sb[:], ADD)
+        for c0, c1, back in old_ps:
+            nc.vector.tensor_tensor(f2[:, c0:c1], f1[:, c0:c1], back[:], ADD)
+        nc.gpsimd.tensor_tensor(f2[:, V_COLS:T], f1[:, V_COLS:T], old_sb[:, V_COLS:T], ADD)
 
         y0 = sb.tile([P, HALF], F32)
         y1 = sb.tile([P, HALF], F32)

@@ -38,13 +38,15 @@ def tile_attend_pairproduct_lean_through_heads_kernel(tc, query, keys_words, key
 
         q_raw = sb.tile([P, PACK, Q], F32, tag="staged", align_bytes=64)
         nc.sync.dma_start(out=q_raw[:], in_=query.rearrange("(p j) q -> p j q", j=PACK))
+        k_words = [sb.tile([P, T], U8, align_bytes=64, name=f"k_words{h}") for h in range(2)]
+        nc.sync.dma_start(out=k_words[0][:].bitcast(I32), in_=keys_words[0, :, 0:T].bitcast(I32))
         for quad in range(4):
-            nc.scalar.dma_start(
+            queue = nc.scalar if quad < 2 else nc.sync
+            queue.dma_start(
                 out=k_scales[32 * quad : 32 * quad + 4, :].bitcast(I32),
                 in_=keys_scales[0, 4 * quad : 4 * quad + 4, :].bitcast(I32),
             )
-        k_words = sb.tile([P, 2 * T], U8, align_bytes=64)
-        nc.sync.dma_start(out=k_words[:].bitcast(I32), in_=keys_words[0].bitcast(I32))
+        nc.sync.dma_start(out=k_words[1][:].bitcast(I32), in_=keys_words[0, :, T : 2 * T].bitcast(I32))
         idx = lists.tile([P, I // 16], U16)
         idx2 = lists.tile([P, I // 16], U16)
         idx3 = lists.tile([P, I // 16], U16)
@@ -80,7 +82,7 @@ def tile_attend_pairproduct_lean_through_heads_kernel(tc, query, keys_words, key
                 out=bank[:],
                 lhsT=q_codes[:].bitcast(FP8X4),
                 lhsT_scale=q_scales[:],
-                rhs=k_words[:, 2 * c0 : 2 * c1].bitcast(FP4X4),
+                rhs=k_words[c0 // 512][:, 2 * (c0 % 512) : 2 * (c0 % 512 + c1 - c0)].bitcast(FP4X4),
                 rhs_scale=k_scales[:, cols],
                 start=True,
                 stop=True,

@@ -1,7 +1,6 @@
 from contextlib import ExitStack
 
 import concourse.mybir as mybir
-from concourse.masks import make_identity
 
 D, T, I, Q = 512, 1024, 512, 128
 FLOPS = 2 * D * Q * T
@@ -21,7 +20,6 @@ ADD = mybir.AluOpType.add
 P = 128
 PACK = 4
 HALF = I // 2
-V_COLS = 768
 
 
 def tile_attend_pairproduct_lean_through_heads_kernel(tc, query, keys_words, keys_scales, old, offs, offs2, offs3, out):
@@ -104,25 +102,8 @@ def tile_attend_pairproduct_lean_through_heads_kernel(tc, query, keys_words, key
         nc.vector.tensor_tensor(f1[:].indirect(idx[:, first]), u0[:], v0[:], MULT)
         nc.vector.tensor_tensor(f1[:].indirect(idx[:, second]), u1[:], v1[:], MULT)
 
-        ident = sb.tile([P, P], F32, tag="small", align_bytes=64)
-        make_identity(nc, ident[:])
-        old_t = sb.tile([P, V_COLS], F32)
-        old_ps = []
-        for b, (c0, c1) in enumerate(((0, 512), (512, V_COLS))):
-            turned = psum.tile([P, c1 - c0], F32, name=f"turned{b}", tag=f"bank{b}")
-            for c in range(c0, c1, P):
-                nc.tensor.transpose(turned[:, c - c0 : c - c0 + P], old_sb[:, c : c + P], ident[:])
-            nc.scalar.copy(old_t[:, c0:c1], turned[:])
-        for b, (c0, c1) in enumerate(((0, 512), (512, V_COLS))):
-            back = psum.tile([P, c1 - c0], F32, name=f"back{b}", tag=f"bank{2 + b}")
-            for c in range(c0, c1, P):
-                nc.tensor.transpose(back[:, c - c0 : c - c0 + P], old_t[:, c : c + P], ident[:])
-            old_ps.append((c0, c1, back))
-
         f2 = sb.tile([P, T], F32)
-        for c0, c1, back in old_ps:
-            nc.vector.tensor_tensor(f2[:, c0:c1], f1[:, c0:c1], back[:], ADD)
-        nc.gpsimd.tensor_tensor(f2[:, V_COLS:T], f1[:, V_COLS:T], old_sb[:, V_COLS:T], ADD)
+        nc.vector.tensor_tensor(f2[:], f1[:], old_sb[:], ADD)
 
         y0 = sb.tile([P, HALF], F32)
         y1 = sb.tile([P, HALF], F32)

from contextlib import ExitStack

import concourse.mybir as mybir

D, T, I, Q = 512, 1024, 512, 128
FLOPS = 2 * D * Q * T

F32 = mybir.dt.float32
BF16 = mybir.dt.bfloat16
I32 = mybir.dt.int32
U32 = mybir.dt.uint32
U16 = mybir.dt.uint16
U8 = mybir.dt.uint8
FP8X4 = mybir.dt.float8_e4m3fn_x4
FP4X4 = mybir.dt.float4_e2m1fn_x4
COPY = mybir.ActivationFunctionType.Copy
MULT = mybir.AluOpType.mult
ADD = mybir.AluOpType.add

P = 128
PACK = 4
HALF = I // 2


def tile_attend_pairproduct_lean_through_heads_kernel(tc, query, keys_words, keys_scales, old, offs, offs2, offs3, out):
    nc = tc.nc
    with ExitStack() as ctx:
        lists = ctx.enter_context(tc.tile_pool(name="lists", bufs=1))
        sb = ctx.enter_context(tc.tile_pool(name="sb", bufs=1))
        psum = ctx.enter_context(tc.psum_pool(name="psum", bufs=1))

        k_scales = sb.tile([P, T], U8, align_bytes=64)
        nc.vector.memset(k_scales[:].bitcast(I32), 0)
        f1 = sb.tile([P, T], F32)
        nc.vector.memset(f1[:], 0.0)

        q_raw = sb.tile([P, PACK, Q], F32, tag="staged", align_bytes=64)
        nc.sync.dma_start(out=q_raw[:], in_=query.rearrange("(p j) q -> p j q", j=PACK))
        k_words = [sb.tile([P, T], U8, align_bytes=64, name=f"k_words{h}") for h in range(2)]
        nc.sync.dma_start(out=k_words[0][:].bitcast(I32), in_=keys_words[0, :, 0:T].bitcast(I32))
        for quad in range(4):
            queue = nc.scalar if quad < 2 else nc.sync
            queue.dma_start(
                out=k_scales[32 * quad : 32 * quad + 4, :].bitcast(I32),
                in_=keys_scales[0, 4 * quad : 4 * quad + 4, :].bitcast(I32),
            )
        nc.sync.dma_start(out=k_words[1][:].bitcast(I32), in_=keys_words[0, :, T : 2 * T].bitcast(I32))
        idx = lists.tile([P, I // 16], U16)
        idx2 = lists.tile([P, I // 16], U16)
        idx3 = lists.tile([P, I // 16], U16)
        nc.sync.dma_start(idx[:], offs)
        nc.sync.dma_start(idx2[:], offs2)
        nc.sync.dma_start(idx3[:], offs3)

        q_bf = sb.tile([P, Q, PACK], BF16, tag="small", align_bytes=64)
        q_codes = sb.tile([P, Q], U32, align_bytes=64)
        q_scales = sb.tile([P, Q], U8, align_bytes=64)
        for h in range(2):
            rows = slice(h * Q // 2, (h + 1) * Q // 2)
            nc.vector.tensor_copy(
                out=q_bf[:, rows, :].rearrange("p (c i) j -> p c j i", i=4),
                in_=q_raw[:, :, rows].rearrange("p j (c i) -> p c j i", i=4),
            )
        for h in range(2):
            rows = slice(h * Q // 2, (h + 1) * Q // 2)
            nc.vector.quantize_mx(
                out=q_codes[:, rows].bitcast(FP8X4),
                scales=q_scales[:, rows],
                in_=q_bf[:, rows, :].rearrange("p q j -> p (q j)"),
            )

        old_sb = sb.tile([P, T], F32, tag="staged", align_bytes=64)
        nc.sync.dma_start(out=old_sb[:], in_=old)

        a = sb.tile([P, T], F32)
        for n, (c0, c1) in enumerate(((0, 256), (256, 512), (512, 768), (768, 896), (896, 1024))):
            cols = slice(c0, c1)
            bank = psum.tile([P, c1 - c0], F32, name=f"bank{n}", tag=f"bank{n}")
            nc.tensor.matmul_mx(
                out=bank[:],
                lhsT=q_codes[:].bitcast(FP8X4),
                lhsT_scale=q_scales[:],
                rhs=k_words[c0 // 512][:, 2 * (c0 % 512) : 2 * (c0 % 512 + c1 - c0)].bitcast(FP4X4),
                rhs_scale=k_scales[:, cols],
                start=True,
                stop=True,
            )
            if n in (0, 2):
                nc.scalar.activation(a[:, cols], bank[:], COPY)
            else:
                nc.vector.tensor_copy(out=a[:, cols], in_=bank[:])

        first, second = slice(0, HALF // 16), slice(HALF // 16, I // 16)
        u0 = sb.tile([P, HALF], F32)
        v0 = sb.tile([P, HALF], F32)
        u1 = sb.tile([P, HALF], F32)
        v1 = sb.tile([P, HALF], F32)
        nc.vector.tensor_copy(u0[:], a[:].indirect(idx[:, first]))
        nc.scalar.activation(v0[:], a[:].indirect(idx2[:, first]), COPY)
        nc.scalar.activation(u1[:], a[:].indirect(idx[:, second]), COPY)
        nc.scalar.activation(v1[:], a[:].indirect(idx2[:, second]), COPY)
        nc.vector.tensor_tensor(f1[:].indirect(idx[:, first]), u0[:], v0[:], MULT)
        nc.vector.tensor_tensor(f1[:].indirect(idx[:, second]), u1[:], v1[:], MULT)

        f2 = sb.tile([P, T], F32)
        nc.vector.tensor_tensor(f2[:], f1[:], old_sb[:], ADD)

        y0 = sb.tile([P, HALF], F32)
        y1 = sb.tile([P, HALF], F32)
        nc.vector.tensor_copy(y0[:], f2[:].indirect(idx3[:, first]))
        nc.scalar.activation(y1[:], f2[:].indirect(idx3[:, second]), COPY)
        nc.sync.dma_start(out=out[:, 0:HALF], in_=y0[:])
        nc.scalar.dma_start(out=out[:, HALF:I], in_=y1[:])
